import numpy as np
import ml_dtypes


def mxq(x, axis, fmt="e4m3"):
    dtype, down = {"e4m3": (ml_dtypes.float8_e4m3fn, 7), "e5m2": (ml_dtypes.float8_e5m2, 14)}[fmt]
    v = np.moveaxis(np.asarray(x, np.float32).astype(ml_dtypes.bfloat16).astype(np.float64), axis, -1)
    blocks = v.reshape(v.shape[:-1] + (-1, 32))
    amax = np.abs(blocks).max(-1, keepdims=True)
    byte = np.maximum(np.where(amax > 0, np.frexp(amax)[1] - 1 + 127, 0) - down, 1)
    scale = np.exp2(byte - 127.0)
    codes = (blocks / scale).astype(np.float32).astype(dtype).astype(np.float64)
    return np.moveaxis((codes * scale).reshape(v.shape), -1, axis)


WIDE = False


def mx_kscale(k):
    if not WIDE:
        return np.ones(k)
    levels = np.array([10, -10, 5, -5, 0])
    if k % 512:
        return np.exp2(np.random.permutation(np.resize(levels, k // 32))).repeat(32)
    a = np.empty((k // 512, 16))
    for p in range(k // 512):
        a[p, :8] = np.random.permutation(np.resize(levels, 8))
        for g in range(8):
            far = levels[np.abs(levels - a[p, g]) >= 10]
            a[p, g + 8] = far[np.random.randint(len(far))]
    return np.exp2(a.ravel()).repeat(32)


def f64(x):
    return np.asarray(x).astype(np.float64)


def striped8(idx):
    return np.asarray(idx).reshape(8, -1, 16).transpose(0, 2, 1).reshape(128, -1).astype(np.uint16)


def unstriped8(offs):
    return offs.reshape(8, 16, -1).transpose(0, 2, 1).reshape(8, -1).astype(np.int64)


def pick8(x, idx, run):
    r = np.arange(len(x))
    return x[r[:, None], idx[r % (8 * run) // run]]


E2M1 = np.array([0.0, 0.5, 1.0, 1.5, 2.0, 3.0, 4.0, 6.0, -0.0, -0.5, -1.0, -1.5, -2.0, -3.0, -4.0, -6.0])


def pack_weight(w, fmt):
    k, n = w.shape
    w = f64(np.asarray(w, np.float32).astype(ml_dtypes.bfloat16)).reshape(k // 32, 32, n)
    amax = np.abs(w).max(1)
    if fmt == "e4m3":
        byte = np.frexp(amax)[1] - 1 + 127 - 7
    else:
        mant, ex = np.frexp(amax / 6.0)
        byte = np.where(mant > 0.5, ex, ex - 1) + 127
    byte = np.clip(np.where(amax > 0, byte, 1), 1, 254)
    scaled = (w * np.exp2(127.0 - byte)[:, None, :]).reshape(k, n).astype(np.float32)
    by_word = np.ascontiguousarray(scaled.reshape(k // 512, 128, 4, n).transpose(0, 1, 3, 2))
    if fmt == "e4m3":
        words = by_word.astype(ml_dtypes.float8_e4m3fn).view(np.uint8)
    else:
        c = by_word.astype(ml_dtypes.float4_e2m1fn).view(np.uint8) & 0xF
        words = (c[..., 0::2] | (c[..., 1::2] << 4)).reshape(k // 512, 128, 2 * n)
    return np.ascontiguousarray(words), np.ascontiguousarray(byte.astype(np.uint8).reshape(k // 512, 16, n))


def unpack_weight(words, scales, fmt):
    g, _, n = scales.shape
    words = np.ascontiguousarray(words).reshape(g, 128, n, -1)
    if fmt == "e4m3":
        vals = words.view(ml_dtypes.float8_e4m3fn).astype(np.float64)
    else:
        nib = np.empty((g, 128, n, 4), np.uint8)
        nib[..., 0::2] = words & 0xF
        nib[..., 1::2] = words >> 4
        vals = E2M1[nib]
    vals = vals * np.repeat(np.exp2(scales.astype(np.float64) - 127.0), 8, axis=1)[..., None]
    return vals.transpose(0, 1, 3, 2).reshape(g * 512, n)


D, T, U, X, I, Q = 512, 1024, 1024, 1024, 512, 128


def setup_inputs():
    n = np.random.standard_normal
    idx = np.stack([np.random.permutation(T)[:I] for _ in range(8)])
    idx2 = np.stack([np.random.permutation(U)[:I] for _ in range(8)])
    idx3 = np.stack([np.random.permutation(X)[:I] for _ in range(8)])
    idx4 = np.stack([np.random.permutation(X)[:I] for _ in range(8)])
    idx5 = np.stack([np.random.permutation(T)[:I] for _ in range(8)])
    fd = mx_kscale(D)
    keysp = pack_weight(n((D, T)) / fd[:, None], "e4m3")
    notesp = pack_weight(n((D, U)) / fd[:, None], "e2m1")
    usersp = pack_weight(n((D, X)) / fd[:, None], "e4m3")
    return {
        "query": (n((D, Q)) * 1.0 / np.sqrt(D) * fd[:, None]).astype(np.float32),
        "keys_words": keysp[0],
        "keys_scales": keysp[1],
        "notes_words": notesp[0],
        "notes_scales": notesp[1],
        "users_words": usersp[0],
        "users_scales": usersp[1],
        "offs": striped8(idx),
        "offs2": striped8(idx2),
        "offs3": striped8(idx3),
        "offs4": striped8(idx4),
        "offs5": striped8(idx5),
    }


def reference(query, keys_words, keys_scales, notes_words, notes_scales, users_words, users_scales, offs, offs2, offs3, offs4, offs5):
    idx = unstriped8(offs)
    idx2 = unstriped8(offs2)
    idx3 = unstriped8(offs3)
    idx4 = unstriped8(offs4)
    idx5 = unstriped8(offs5)
    keysu = unpack_weight(keys_words, keys_scales, "e4m3")
    notesu = unpack_weight(notes_words, notes_scales, "e2m1")
    usersu = unpack_weight(users_words, users_scales, "e4m3")
    queryq = mxq(f64(query), 0, "e4m3")
    a = queryq.T @ keysu
    b = queryq.T @ notesu
    c0 = queryq.T @ usersu
    hi1 = np.maximum(np.maximum(pick8(a, idx, 16), pick8(b, idx2, 16)), pick8(c0, idx3, 16))
    lo1 = np.minimum(np.minimum(pick8(a, idx, 16), pick8(b, idx2, 16)), pick8(c0, idx3, 16))
    r = hi1 - lo1
    f1 = np.zeros((Q, X))
    f1[np.arange(Q)[:, None], idx4[np.arange(Q) % 128 // 16]] = r
    cc = c0 - f1
    v = pick8(cc, idx3, 16) + lo1
    y = np.maximum(v, pick8(a, idx5, 16))
    return y

@@ -1,0 +1,125 @@
+from contextlib import ExitStack
+
+import concourse.mybir as mybir
+
+F32 = mybir.dt.float32
+BF16 = mybir.dt.bfloat16
+I32 = mybir.dt.int32
+U32 = mybir.dt.uint32
+U16 = mybir.dt.uint16
+U8 = mybir.dt.uint8
+FP8X4 = mybir.dt.float8_e4m3fn_x4
+FP4X4 = mybir.dt.float4_e2m1fn_x4
+ALU = mybir.AluOpType
+COPY = mybir.ActivationFunctionType.Copy
+
+P = 128
+PACK = 4
+Q = 128
+POOL = 1024
+SLOTS = 512
+BANK = 512
+HALF = SLOTS // 2
+FLOPS = 2 * 512 * Q * 3 * POOL
+
+
+def tile_attend_rangeof_three_kernel(tc, query, keys_words, keys_scales, notes_words, notes_scales,
+                                      users_words, users_scales, offs, offs2, offs3, offs4, offs5, out):
+    nc = tc.nc
+    with ExitStack() as ctx:
+        sb = ctx.enter_context(tc.tile_pool(name="sb", bufs=1))
+        psum = ctx.enter_context(tc.psum_pool(name="psum", bufs=1))
+
+        def load_plane(queue, plane, scales):
+            for r in range(4):
+                queue.dma_start(plane[r:P:32, :].bitcast(I32), scales[0][r:16:4, :].bitcast(I32))
+
+        def load_list(src, name):
+            t = sb.tile([P, SLOTS // 16], U16, name=name)
+            nc.sync.dma_start(t[:], src)
+            return t
+
+        n_plane = sb.tile([P, POOL], U8, align_bytes=64)
+        u_plane = sb.tile([P, POOL], U8, align_bytes=64)
+        k_plane = sb.tile([P, POOL], U8, align_bytes=64)
+        f1 = sb.tile([P, POOL], F32)
+        for plane in (n_plane, u_plane, k_plane):
+            nc.vector.memset(plane[:].bitcast(I32), 0)
+        nc.vector.memset(f1[:], 0.0)
+
+        q_raw = sb.tile([P, PACK, Q], F32)
+        n_words = sb.tile([P, 2 * POOL], U8, align_bytes=64)
+        u_words = sb.tile([P, POOL], U32, align_bytes=64)
+        k_words = sb.tile([P, POOL], U32, align_bytes=64)
+        nc.sync.dma_start(q_raw[:], query.rearrange("(p t) q -> p t q", t=PACK))
+        load_plane(nc.scalar, n_plane, notes_scales)
+        nc.sync.dma_start(n_words[:].bitcast(I32), notes_words[0].bitcast(I32))
+        nc.sync.dma_start(u_words[:].bitcast(I32), users_words[0].rearrange("p n t -> p (n t)").bitcast(I32))
+        idx2 = load_list(offs2, "idx2")
+        load_plane(nc.scalar, u_plane, users_scales)
+        load_plane(nc.gpsimd, k_plane, keys_scales)
+        nc.sync.dma_start(k_words[:].bitcast(I32), keys_words[0].rearrange("p n t -> p (n t)").bitcast(I32))
+        idx3 = load_list(offs3, "idx3")
+        idx = load_list(offs, "idx")
+        idx4 = load_list(offs4, "idx4")
+        idx5 = load_list(offs5, "idx5")
+
+        q_bf = sb.tile([P, Q, PACK], BF16, align_bytes=64)
+        q_words = sb.tile([P, Q], U32, align_bytes=64)
+        q_plane = sb.tile([P, Q], U8, align_bytes=64)
+        nc.vector.tensor_copy(q_bf[:], q_raw[:].rearrange("p t q -> p q t"))
+        nc.vector.quantize_mx(out=q_words[:].bitcast(FP8X4), scales=q_plane[:],
+                              in_=q_bf[:].rearrange("p q t -> p (q t)"))
+
+        def scores(moving, plane, half, name):
+            bank = psum.tile([Q, BANK], F32, name=name)
+            nc.tensor.matmul_mx(out=bank[:], lhsT=q_words[:].bitcast(FP8X4), lhsT_scale=q_plane[:],
+                                rhs=moving, rhs_scale=plane[:, half * BANK:(half + 1) * BANK],
+                                start=True, stop=True)
+            return bank
+
+        a = sb.tile([P, POOL], F32)
+        b = sb.tile([P, POOL], F32)
+        c0 = sb.tile([P, POOL], F32)
+        lo_cols = slice(0, BANK)
+        hi_cols = slice(BANK, POOL)
+        b_banks = [scores(n_words[:, 2 * h * BANK:2 * (h + 1) * BANK].bitcast(FP4X4), n_plane, h, "b%d" % h) for h in range(2)]
+        c_banks = [scores(u_words[:, h * BANK:(h + 1) * BANK].bitcast(FP8X4), u_plane, h, "c%d" % h) for h in range(2)]
+        a_banks = [scores(k_words[:, h * BANK:(h + 1) * BANK].bitcast(FP8X4), k_plane, h, "a%d" % h) for h in range(2)]
+
+        nc.vector.tensor_copy(b[:, lo_cols], b_banks[0][:])
+        nc.scalar.copy(b[:, hi_cols], b_banks[1][:])
+        b_sel = sb.tile([P, SLOTS], F32)
+        nc.vector.tensor_copy(b_sel[:], b[:].indirect(idx2[:]))
+        nc.scalar.copy(c0[:, lo_cols], c_banks[0][:])
+        nc.scalar.copy(c0[:, hi_cols], c_banks[1][:])
+        c_neg = sb.tile([P, SLOTS], F32)
+        nc.scalar.activation(c_neg[:], c0[:].indirect(idx3[:]), COPY, scale=-1.0)
+        nc.vector.tensor_copy(a[:, lo_cols], a_banks[0][:])
+        nc.vector.tensor_copy(a[:, hi_cols], a_banks[1][:])
+        a_sel = sb.tile([P, SLOTS], F32)
+        nc.scalar.activation(a_sel[:], a[:].indirect(idx[:]), COPY)
+        a5 = sb.tile([P, SLOTS], F32)
+        nc.scalar.activation(a5[:], a[:].indirect(idx5[:]), COPY)
+
+        bc_hi = sb.tile([P, SLOTS], F32)
+        bc_nlo = sb.tile([P, SLOTS], F32)
+        hi1 = sb.tile([P, SLOTS], F32)
+        nlo1 = sb.tile([P, SLOTS], F32)
+        nc.vector.scalar_tensor_tensor(bc_hi[:], c_neg[:], -1.0, b_sel[:], ALU.mult, ALU.max)
+        nc.vector.scalar_tensor_tensor(bc_nlo[:], b_sel[:], -1.0, c_neg[:], ALU.mult, ALU.max)
+        nc.vector.tensor_tensor(hi1[:], a_sel[:], bc_hi[:], ALU.max)
+        nc.vector.scalar_tensor_tensor(nlo1[:], a_sel[:], -1.0, bc_nlo[:], ALU.mult, ALU.max)
+        nc.vector.tensor_tensor(f1[:].indirect(idx4[:]), hi1[:], nlo1[:], ALU.add)
+        cc = sb.tile([P, POOL], F32)
+        nc.vector.tensor_tensor(cc[:], c0[:], f1[:], ALU.subtract)
+
+        v = sb.tile([P, SLOTS], F32)
+        y = sb.tile([P, SLOTS], F32)
+        for h in range(2):
+            s = slice(h * HALF, (h + 1) * HALF)
+            nc.vector.tensor_tensor(v[:, s], cc[:].indirect(idx3[:, h * HALF // 16:(h + 1) * HALF // 16]), nlo1[:, s], ALU.subtract)
+        for h, queue in enumerate((nc.sync, nc.scalar)):
+            s = slice(h * HALF, (h + 1) * HALF)
+            nc.vector.tensor_tensor(y[:, s], v[:, s], a5[:, s], ALU.max)
+            queue.dma_start(out[:, s], y[:, s])

@@ -52,13 +52,13 @@ def tile_attend_rangeof_three_kernel(tc, query, keys_words, keys_scales, notes_w
         u_words = sb.tile([P, POOL], U32, align_bytes=64)
         k_words = sb.tile([P, POOL], U32, align_bytes=64)
         nc.sync.dma_start(q_raw[:], query.rearrange("(p t) q -> p t q", t=PACK))
-        load_plane(nc.scalar, n_plane, notes_scales)
         nc.sync.dma_start(n_words[:].bitcast(I32), notes_words[0].bitcast(I32))
-        nc.sync.dma_start(u_words[:].bitcast(I32), users_words[0].rearrange("p n t -> p (n t)").bitcast(I32))
         idx2 = load_list(offs2, "idx2")
-        load_plane(nc.scalar, u_plane, users_scales)
-        load_plane(nc.gpsimd, k_plane, keys_scales)
+        load_plane(nc.sync, n_plane, notes_scales)
+        nc.sync.dma_start(u_words[:].bitcast(I32), users_words[0].rearrange("p n t -> p (n t)").bitcast(I32))
+        load_plane(nc.sync, u_plane, users_scales)
         nc.sync.dma_start(k_words[:].bitcast(I32), keys_words[0].rearrange("p n t -> p (n t)").bitcast(I32))
+        load_plane(nc.sync, k_plane, keys_scales)
         idx3 = load_list(offs3, "idx3")
         idx = load_list(offs, "idx")
         idx4 = load_list(offs4, "idx4")
@@ -87,18 +87,26 @@ def tile_attend_rangeof_three_kernel(tc, query, keys_words, keys_scales, notes_w
         c_banks = [scores(u_words[:, h * BANK:(h + 1) * BANK].bitcast(FP8X4), u_plane, h, "c%d" % h) for h in range(2)]
         a_banks = [scores(k_words[:, h * BANK:(h + 1) * BANK].bitcast(FP8X4), k_plane, h, "a%d" % h) for h in range(2)]
 
+        halves = [slice(h * HALF, (h + 1) * HALF) for h in range(2)]
+
+        def half_list(t, h):
+            return t[:, h * HALF // 16:(h + 1) * HALF // 16]
+
+        s0, s1 = halves
         nc.vector.tensor_copy(b[:, lo_cols], b_banks[0][:])
         nc.scalar.copy(b[:, hi_cols], b_banks[1][:])
-        b_sel = sb.tile([P, SLOTS], F32)
-        nc.vector.tensor_copy(b_sel[:], b[:].indirect(idx2[:]))
-        nc.scalar.copy(c0[:, lo_cols], c_banks[0][:])
-        nc.scalar.copy(c0[:, hi_cols], c_banks[1][:])
-        c_neg = sb.tile([P, SLOTS], F32)
-        nc.scalar.activation(c_neg[:], c0[:].indirect(idx3[:]), COPY, scale=-1.0)
+        b_neg = sb.tile([P, SLOTS], F32)
+        nc.scalar.activation(b_neg[:], b[:].indirect(idx2[:]), COPY, scale=-1.0)
+        nc.vector.tensor_copy(c0[:, lo_cols], c_banks[0][:])
+        nc.vector.tensor_copy(c0[:, hi_cols], c_banks[1][:])
+        c_sel = sb.tile([P, SLOTS], F32)
+        nc.vector.tensor_copy(c_sel[:, s0], c0[:].indirect(half_list(idx3, 0)))
+        nc.scalar.activation(c_sel[:, s1], c0[:].indirect(half_list(idx3, 1)), COPY)
         nc.vector.tensor_copy(a[:, lo_cols], a_banks[0][:])
-        nc.vector.tensor_copy(a[:, hi_cols], a_banks[1][:])
+        nc.scalar.copy(a[:, hi_cols], a_banks[1][:])
         a_sel = sb.tile([P, SLOTS], F32)
-        nc.scalar.activation(a_sel[:], a[:].indirect(idx[:]), COPY)
+        for h, s in enumerate(halves):
+            nc.scalar.activation(a_sel[:, s], a[:].indirect(half_list(idx, h)), COPY)
         a5 = sb.tile([P, SLOTS], F32)
         nc.scalar.activation(a5[:], a[:].indirect(idx5[:]), COPY)
 
@@ -106,20 +114,21 @@ def tile_attend_rangeof_three_kernel(tc, query, keys_words, keys_scales, notes_w
         bc_nlo = sb.tile([P, SLOTS], F32)
         hi1 = sb.tile([P, SLOTS], F32)
         nlo1 = sb.tile([P, SLOTS], F32)
-        nc.vector.scalar_tensor_tensor(bc_hi[:], c_neg[:], -1.0, b_sel[:], ALU.mult, ALU.max)
-        nc.vector.scalar_tensor_tensor(bc_nlo[:], b_sel[:], -1.0, c_neg[:], ALU.mult, ALU.max)
-        nc.vector.tensor_tensor(hi1[:], a_sel[:], bc_hi[:], ALU.max)
-        nc.vector.scalar_tensor_tensor(nlo1[:], a_sel[:], -1.0, bc_nlo[:], ALU.mult, ALU.max)
+        nc.vector.scalar_tensor_tensor(bc_hi[:], b_neg[:], -1.0, c_sel[:], ALU.mult, ALU.max)
+        nc.vector.scalar_tensor_tensor(bc_nlo[:], c_sel[:], -1.0, b_neg[:], ALU.mult, ALU.max)
+        for s in halves:
+            nc.vector.tensor_tensor(hi1[:, s], a_sel[:, s], bc_hi[:, s], ALU.max)
+            nc.vector.scalar_tensor_tensor(nlo1[:, s], a_sel[:, s], -1.0, bc_nlo[:, s], ALU.mult, ALU.max)
         nc.vector.tensor_tensor(f1[:].indirect(idx4[:]), hi1[:], nlo1[:], ALU.add)
         cc = sb.tile([P, POOL], F32)
         nc.vector.tensor_tensor(cc[:], c0[:], f1[:], ALU.subtract)
 
         v = sb.tile([P, SLOTS], F32)
         y = sb.tile([P, SLOTS], F32)
-        for h in range(2):
-            s = slice(h * HALF, (h + 1) * HALF)
-            nc.vector.tensor_tensor(v[:, s], cc[:].indirect(idx3[:, h * HALF // 16:(h + 1) * HALF // 16]), nlo1[:, s], ALU.subtract)
-        for h, queue in enumerate((nc.sync, nc.scalar)):
-            s = slice(h * HALF, (h + 1) * HALF)
+        cc_sel = sb.tile([P, HALF], F32)
+        nc.vector.tensor_tensor(v[:, s0], cc[:].indirect(half_list(idx3, 0)), nlo1[:, s0], ALU.subtract)
+        nc.scalar.activation(cc_sel[:], cc[:].indirect(half_list(idx3, 1)), COPY)
+        nc.vector.tensor_tensor(v[:, s1], cc_sel[:], nlo1[:, s1], ALU.subtract)
+        for s, queue in zip(halves, (nc.sync, nc.scalar)):
             nc.vector.tensor_tensor(y[:, s], v[:, s], a5[:, s], ALU.max)
             queue.dma_start(out[:, s], y[:, s])

@@ -30,8 +30,8 @@ def tile_attend_rangeof_three_kernel(tc, query, keys_words, keys_scales, notes_w
         sb = ctx.enter_context(tc.tile_pool(name="sb", bufs=1))
         psum = ctx.enter_context(tc.psum_pool(name="psum", bufs=1))
 
-        def load_plane(queue, plane, scales):
-            for r in range(4):
+        def load_plane(queue, plane, scales, rows):
+            for r in rows:
                 queue.dma_start(plane[r:P:32, :].bitcast(I32), scales[0][r:16:4, :].bitcast(I32))
 
         def load_list(src, name):
@@ -42,40 +42,42 @@ def tile_attend_rangeof_three_kernel(tc, query, keys_words, keys_scales, notes_w
         n_plane = sb.tile([P, POOL], U8, align_bytes=64)
         u_plane = sb.tile([P, POOL], U8, align_bytes=64)
         k_plane = sb.tile([P, POOL], U8, align_bytes=64)
-        f1 = sb.tile([P, POOL], F32)
         for plane in (n_plane, u_plane, k_plane):
             nc.vector.memset(plane[:].bitcast(I32), 0)
-        nc.vector.memset(f1[:], 0.0)
 
         q_raw = sb.tile([P, PACK, Q], F32)
         n_words = sb.tile([P, 2 * POOL], U8, align_bytes=64)
         u_words = sb.tile([P, POOL], U32, align_bytes=64)
-        k_words = sb.tile([P, POOL], U32, align_bytes=64)
+        k_words = sb.tile([P, POOL], U32, align_bytes=64, tag="keys_then_bc")
         nc.sync.dma_start(q_raw[:], query.rearrange("(p t) q -> p t q", t=PACK))
+        load_plane(nc.sync, n_plane, notes_scales, (0, 1))
+        load_plane(nc.scalar, n_plane, notes_scales, (2, 3))
         nc.sync.dma_start(n_words[:].bitcast(I32), notes_words[0].bitcast(I32))
-        idx2 = load_list(offs2, "idx2")
-        load_plane(nc.sync, n_plane, notes_scales)
+        load_plane(nc.scalar, u_plane, users_scales, (0,))
         nc.sync.dma_start(u_words[:].bitcast(I32), users_words[0].rearrange("p n t -> p (n t)").bitcast(I32))
-        load_plane(nc.sync, u_plane, users_scales)
+        load_plane(nc.sync, u_plane, users_scales, (1, 2, 3))
+        idx2 = load_list(offs2, "idx2")
         nc.sync.dma_start(k_words[:].bitcast(I32), keys_words[0].rearrange("p n t -> p (n t)").bitcast(I32))
-        load_plane(nc.sync, k_plane, keys_scales)
         idx3 = load_list(offs3, "idx3")
+        load_plane(nc.sync, k_plane, keys_scales, (0, 1, 2, 3))
         idx = load_list(offs, "idx")
         idx4 = load_list(offs4, "idx4")
         idx5 = load_list(offs5, "idx5")
 
-        q_bf = sb.tile([P, Q, PACK], BF16, align_bytes=64)
+        q_bf = sb.tile([P, Q, PACK], BF16, align_bytes=64, tag="q_then_f1")
         q_words = sb.tile([P, Q], U32, align_bytes=64)
         q_plane = sb.tile([P, Q], U8, align_bytes=64)
         nc.vector.tensor_copy(q_bf[:], q_raw[:].rearrange("p t q -> p q t"))
         nc.vector.quantize_mx(out=q_words[:].bitcast(FP8X4), scales=q_plane[:],
                               in_=q_bf[:].rearrange("p q t -> p (q t)"))
 
-        def scores(moving, plane, half, name):
-            bank = psum.tile([Q, BANK], F32, name=name)
+        f1 = sb.tile([P, POOL], F32, align_bytes=64, tag="q_then_f1")
+        nc.vector.memset(f1[:], 0.0)
+
+        def scores(moving, moving_plane, name):
+            bank = psum.tile([Q, moving_plane.shape[1]], F32, name=name)
             nc.tensor.matmul_mx(out=bank[:], lhsT=q_words[:].bitcast(FP8X4), lhsT_scale=q_plane[:],
-                                rhs=moving, rhs_scale=plane[:, half * BANK:(half + 1) * BANK],
-                                start=True, stop=True)
+                                rhs=moving, rhs_scale=moving_plane, start=True, stop=True)
             return bank
 
         a = sb.tile([P, POOL], F32)
@@ -83,9 +85,10 @@ def tile_attend_rangeof_three_kernel(tc, query, keys_words, keys_scales, notes_w
         c0 = sb.tile([P, POOL], F32)
         lo_cols = slice(0, BANK)
         hi_cols = slice(BANK, POOL)
-        b_banks = [scores(n_words[:, 2 * h * BANK:2 * (h + 1) * BANK].bitcast(FP4X4), n_plane, h, "b%d" % h) for h in range(2)]
-        c_banks = [scores(u_words[:, h * BANK:(h + 1) * BANK].bitcast(FP8X4), u_plane, h, "c%d" % h) for h in range(2)]
-        a_banks = [scores(k_words[:, h * BANK:(h + 1) * BANK].bitcast(FP8X4), k_plane, h, "a%d" % h) for h in range(2)]
+        b_cols = [slice(0, 512), slice(512, 768), slice(768, 1024)]
+        b_banks = [scores(n_words[:, 2 * s.start:2 * s.stop].bitcast(FP4X4), n_plane[:, s], "b%d" % s.start) for s in b_cols]
+        c_banks = [scores(u_words[:, s].bitcast(FP8X4), u_plane[:, s], "c%d" % s.start) for s in (lo_cols, hi_cols)]
+        a_banks = [scores(k_words[:, s].bitcast(FP8X4), k_plane[:, s], "a%d" % s.start) for s in (lo_cols, hi_cols)]
 
         halves = [slice(h * HALF, (h + 1) * HALF) for h in range(2)]
 
@@ -93,42 +96,45 @@ def tile_attend_rangeof_three_kernel(tc, query, keys_words, keys_scales, notes_w
             return t[:, h * HALF // 16:(h + 1) * HALF // 16]
 
         s0, s1 = halves
-        nc.vector.tensor_copy(b[:, lo_cols], b_banks[0][:])
-        nc.scalar.copy(b[:, hi_cols], b_banks[1][:])
-        b_neg = sb.tile([P, SLOTS], F32)
-        nc.scalar.activation(b_neg[:], b[:].indirect(idx2[:]), COPY, scale=-1.0)
-        nc.vector.tensor_copy(c0[:, lo_cols], c_banks[0][:])
-        nc.vector.tensor_copy(c0[:, hi_cols], c_banks[1][:])
-        c_sel = sb.tile([P, SLOTS], F32)
-        nc.vector.tensor_copy(c_sel[:, s0], c0[:].indirect(half_list(idx3, 0)))
-        nc.scalar.activation(c_sel[:, s1], c0[:].indirect(half_list(idx3, 1)), COPY)
+        nc.vector.tensor_copy(b[:, b_cols[0]], b_banks[0][:])
+        nc.scalar.copy(b[:, b_cols[1]], b_banks[1][:])
+        nc.vector.tensor_copy(b[:, b_cols[2]], b_banks[2][:])
+        b_sel = sb.tile([P, SLOTS], F32)
+        nc.vector.tensor_copy(b_sel[:], b[:].indirect(idx2[:]))
+        nc.scalar.copy(c0[:, lo_cols], c_banks[0][:])
+        nc.scalar.copy(c0[:, hi_cols], c_banks[1][:])
+        c_sel = [sb.tile([P, HALF], F32, name="c_sel%d" % h) for h in range(2)]
+        nc.vector.tensor_copy(c_sel[0][:], c0[:].indirect(half_list(idx3, 0)))
+        nc.scalar.activation(c_sel[1][:], c0[:].indirect(half_list(idx3, 1)), COPY)
         nc.vector.tensor_copy(a[:, lo_cols], a_banks[0][:])
         nc.scalar.copy(a[:, hi_cols], a_banks[1][:])
-        a_sel = sb.tile([P, SLOTS], F32)
+        a_neg = [sb.tile([P, HALF], F32, name="a_neg%d" % h) for h in range(2)]
         for h, s in enumerate(halves):
-            nc.scalar.activation(a_sel[:, s], a[:].indirect(half_list(idx, h)), COPY)
+            nc.scalar.activation(a_neg[h][:], a[:].indirect(half_list(idx, h)), COPY, scale=-1.0)
         a5 = sb.tile([P, SLOTS], F32)
         nc.scalar.activation(a5[:], a[:].indirect(idx5[:]), COPY)
 
-        bc_hi = sb.tile([P, SLOTS], F32)
-        bc_nlo = sb.tile([P, SLOTS], F32)
+        bc = sb.tile([P, 2 * SLOTS], F32, align_bytes=64, tag="keys_then_bc")
+        bc_hi = bc[:, 0:SLOTS]
+        bc_lo = bc[:, SLOTS:2 * SLOTS]
         hi1 = sb.tile([P, SLOTS], F32)
         nlo1 = sb.tile([P, SLOTS], F32)
-        nc.vector.scalar_tensor_tensor(bc_hi[:], b_neg[:], -1.0, c_sel[:], ALU.mult, ALU.max)
-        nc.vector.scalar_tensor_tensor(bc_nlo[:], c_sel[:], -1.0, b_neg[:], ALU.mult, ALU.max)
-        for s in halves:
-            nc.vector.tensor_tensor(hi1[:, s], a_sel[:, s], bc_hi[:, s], ALU.max)
-            nc.vector.scalar_tensor_tensor(nlo1[:, s], a_sel[:, s], -1.0, bc_nlo[:, s], ALU.mult, ALU.max)
+        for h, s in enumerate(halves):
+            nc.vector.tensor_tensor(bc_hi[:, s], b_sel[:, s], c_sel[h][:], ALU.max)
+            nc.vector.tensor_tensor(bc_lo[:, s], b_sel[:, s], c_sel[h][:], ALU.min)
+        for h, s in enumerate(halves):
+            nc.vector.scalar_tensor_tensor(hi1[:, s], a_neg[h][:], -1.0, bc_hi[:, s], ALU.mult, ALU.max)
+            nc.vector.scalar_tensor_tensor(nlo1[:, s], bc_lo[:, s], -1.0, a_neg[h][:], ALU.mult, ALU.max)
         nc.vector.tensor_tensor(f1[:].indirect(idx4[:]), hi1[:], nlo1[:], ALU.add)
-        cc = sb.tile([P, POOL], F32)
+        cc = sb.tile([P, POOL], F32, tag="cc_then_y")
         nc.vector.tensor_tensor(cc[:], c0[:], f1[:], ALU.subtract)
 
-        v = sb.tile([P, SLOTS], F32)
-        y = sb.tile([P, SLOTS], F32)
         cc_sel = sb.tile([P, HALF], F32)
+        v = sb.tile([P, SLOTS], F32)
         nc.vector.tensor_tensor(v[:, s0], cc[:].indirect(half_list(idx3, 0)), nlo1[:, s0], ALU.subtract)
         nc.scalar.activation(cc_sel[:], cc[:].indirect(half_list(idx3, 1)), COPY)
         nc.vector.tensor_tensor(v[:, s1], cc_sel[:], nlo1[:, s1], ALU.subtract)
+        y = sb.tile([P, SLOTS], F32, tag="cc_then_y")
         for s, queue in zip(halves, (nc.sync, nc.scalar)):
             nc.vector.tensor_tensor(y[:, s], v[:, s], a5[:, s], ALU.max)
             queue.dma_start(out[:, s], y[:, s])

from contextlib import ExitStack

import concourse.mybir as mybir

F32 = mybir.dt.float32
BF16 = mybir.dt.bfloat16
I32 = mybir.dt.int32
U32 = mybir.dt.uint32
U16 = mybir.dt.uint16
U8 = mybir.dt.uint8
FP8X4 = mybir.dt.float8_e4m3fn_x4
FP4X4 = mybir.dt.float4_e2m1fn_x4
ALU = mybir.AluOpType
COPY = mybir.ActivationFunctionType.Copy

P = 128
PACK = 4
Q = 128
POOL = 1024
SLOTS = 512
BANK = 512
HALF = SLOTS // 2
FLOPS = 2 * 512 * Q * 3 * POOL


def tile_attend_rangeof_three_kernel(tc, query, keys_words, keys_scales, notes_words, notes_scales,
                                      users_words, users_scales, offs, offs2, offs3, offs4, offs5, out):
    nc = tc.nc
    with ExitStack() as ctx:
        sb = ctx.enter_context(tc.tile_pool(name="sb", bufs=1))
        psum = ctx.enter_context(tc.psum_pool(name="psum", bufs=1))

        def load_plane(queue, plane, scales, rows):
            for r in rows:
                queue.dma_start(plane[r:P:32, :].bitcast(I32), scales[0][r:16:4, :].bitcast(I32))

        def load_list(src, name):
            t = sb.tile([P, SLOTS // 16], U16, name=name)
            nc.sync.dma_start(t[:], src)
            return t

        n_plane = sb.tile([P, POOL], U8, align_bytes=64)
        u_plane = sb.tile([P, POOL], U8, align_bytes=64)
        k_plane = sb.tile([P, POOL], U8, align_bytes=64)
        for plane in (n_plane, u_plane, k_plane):
            nc.vector.memset(plane[:].bitcast(I32), 0)

        q_raw = sb.tile([P, PACK, Q], F32)
        n_words = sb.tile([P, 2 * POOL], U8, align_bytes=64)
        u_words = sb.tile([P, POOL], U32, align_bytes=64)
        k_words = sb.tile([P, POOL], U32, align_bytes=64, tag="keys_then_bc")
        nc.sync.dma_start(q_raw[:], query.rearrange("(p t) q -> p t q", t=PACK))
        load_plane(nc.sync, n_plane, notes_scales, (0, 1))
        load_plane(nc.scalar, n_plane, notes_scales, (2, 3))
        nc.sync.dma_start(n_words[:].bitcast(I32), notes_words[0].bitcast(I32))
        load_plane(nc.scalar, u_plane, users_scales, (0,))
        nc.sync.dma_start(u_words[:].bitcast(I32), users_words[0].rearrange("p n t -> p (n t)").bitcast(I32))
        load_plane(nc.sync, u_plane, users_scales, (1, 2, 3))
        idx2 = load_list(offs2, "idx2")
        nc.sync.dma_start(k_words[:].bitcast(I32), keys_words[0].rearrange("p n t -> p (n t)").bitcast(I32))
        idx3 = load_list(offs3, "idx3")
        load_plane(nc.sync, k_plane, keys_scales, (0, 1, 2, 3))
        idx = load_list(offs, "idx")
        idx4 = load_list(offs4, "idx4")
        idx5 = load_list(offs5, "idx5")

        q_bf = sb.tile([P, Q, PACK], BF16, align_bytes=64, tag="q_then_f1")
        q_words = sb.tile([P, Q], U32, align_bytes=64)
        q_plane = sb.tile([P, Q], U8, align_bytes=64)
        nc.vector.tensor_copy(q_bf[:], q_raw[:].rearrange("p t q -> p q t"))
        nc.vector.quantize_mx(out=q_words[:].bitcast(FP8X4), scales=q_plane[:],
                              in_=q_bf[:].rearrange("p q t -> p (q t)"))

        f1 = sb.tile([P, POOL], F32, align_bytes=64, tag="q_then_f1")
        nc.vector.memset(f1[:], 0.0)

        def scores(moving, moving_plane, name):
            bank = psum.tile([Q, moving_plane.shape[1]], F32, name=name)
            nc.tensor.matmul_mx(out=bank[:], lhsT=q_words[:].bitcast(FP8X4), lhsT_scale=q_plane[:],
                                rhs=moving, rhs_scale=moving_plane, start=True, stop=True)
            return bank

        a = sb.tile([P, POOL], F32)
        b = sb.tile([P, POOL], F32)
        c0 = sb.tile([P, POOL], F32)
        lo_cols = slice(0, BANK)
        hi_cols = slice(BANK, POOL)
        b_cols = [slice(0, 512), slice(512, 768), slice(768, 1024)]
        b_banks = [scores(n_words[:, 2 * s.start:2 * s.stop].bitcast(FP4X4), n_plane[:, s], "b%d" % s.start) for s in b_cols]
        c_banks = [scores(u_words[:, s].bitcast(FP8X4), u_plane[:, s], "c%d" % s.start) for s in (lo_cols, hi_cols)]
        a_banks = [scores(k_words[:, s].bitcast(FP8X4), k_plane[:, s], "a%d" % s.start) for s in (lo_cols, hi_cols)]

        halves = [slice(h * HALF, (h + 1) * HALF) for h in range(2)]

        def half_list(t, h):
            return t[:, h * HALF // 16:(h + 1) * HALF // 16]

        s0, s1 = halves
        nc.vector.tensor_copy(b[:, b_cols[0]], b_banks[0][:])
        nc.scalar.copy(b[:, b_cols[1]], b_banks[1][:])
        nc.vector.tensor_copy(b[:, b_cols[2]], b_banks[2][:])
        b_sel = sb.tile([P, SLOTS], F32)
        nc.vector.tensor_copy(b_sel[:], b[:].indirect(idx2[:]))
        nc.scalar.copy(c0[:, lo_cols], c_banks[0][:])
        nc.scalar.copy(c0[:, hi_cols], c_banks[1][:])
        c_sel = [sb.tile([P, HALF], F32, name="c_sel%d" % h) for h in range(2)]
        nc.vector.tensor_copy(c_sel[0][:], c0[:].indirect(half_list(idx3, 0)))
        nc.scalar.activation(c_sel[1][:], c0[:].indirect(half_list(idx3, 1)), COPY)
        nc.vector.tensor_copy(a[:, lo_cols], a_banks[0][:])
        nc.scalar.copy(a[:, hi_cols], a_banks[1][:])
        a_neg = [sb.tile([P, HALF], F32, name="a_neg%d" % h) for h in range(2)]
        for h, s in enumerate(halves):
            nc.scalar.activation(a_neg[h][:], a[:].indirect(half_list(idx, h)), COPY, scale=-1.0)
        a5 = sb.tile([P, SLOTS], F32)
        nc.scalar.activation(a5[:], a[:].indirect(idx5[:]), COPY)

        bc = sb.tile([P, 2 * SLOTS], F32, align_bytes=64, tag="keys_then_bc")
        bc_hi = bc[:, 0:SLOTS]
        bc_lo = bc[:, SLOTS:2 * SLOTS]
        hi1 = sb.tile([P, SLOTS], F32)
        nlo1 = sb.tile([P, SLOTS], F32)
        for h, s in enumerate(halves):
            nc.vector.tensor_tensor(bc_hi[:, s], b_sel[:, s], c_sel[h][:], ALU.max)
            nc.vector.tensor_tensor(bc_lo[:, s], b_sel[:, s], c_sel[h][:], ALU.min)
        for h, s in enumerate(halves):
            nc.vector.scalar_tensor_tensor(hi1[:, s], a_neg[h][:], -1.0, bc_hi[:, s], ALU.mult, ALU.max)
            nc.vector.scalar_tensor_tensor(nlo1[:, s], bc_lo[:, s], -1.0, a_neg[h][:], ALU.mult, ALU.max)
        nc.vector.tensor_tensor(f1[:].indirect(idx4[:]), hi1[:], nlo1[:], ALU.add)
        cc = sb.tile([P, POOL], F32, tag="cc_then_y")
        nc.vector.tensor_tensor(cc[:], c0[:], f1[:], ALU.subtract)

        cc_sel = sb.tile([P, HALF], F32)
        v = sb.tile([P, SLOTS], F32)
        nc.vector.tensor_tensor(v[:, s0], cc[:].indirect(half_list(idx3, 0)), nlo1[:, s0], ALU.subtract)
        nc.scalar.activation(cc_sel[:], cc[:].indirect(half_list(idx3, 1)), COPY)
        nc.vector.tensor_tensor(v[:, s1], cc_sel[:], nlo1[:, s1], ALU.subtract)
        y = sb.tile([P, SLOTS], F32, tag="cc_then_y")
        for s, queue in zip(halves, (nc.sync, nc.scalar)):
            nc.vector.tensor_tensor(y[:, s], v[:, s], a5[:, s], ALU.max)
            queue.dma_start(out[:, s], y[:, s])
